import numpy as np, ml_dtypes
CORES = [9,17,137,145,265,273,393,401]
N = 8
NB, B = 6, 64
def setup_inputs(rng):
    return {"x": rng.standard_normal((N, 128, NB * B), dtype=np.float32).astype(ml_dtypes.bfloat16), "wv": (rng.standard_normal((N, 128, 128), dtype=np.float32) / 16).astype(ml_dtypes.bfloat16), "wh": (rng.standard_normal((N, 128, 128), dtype=np.float32) / 16).astype(ml_dtypes.bfloat16)}
def setup_inputs_big(rng):
    d = setup_inputs(rng)
    for k in ("x",): d[k] = (d[k].astype(np.float32) * 1048576.0).astype(d[k].dtype)
    return d
def setup_inputs_small(rng):
    d = setup_inputs(rng)
    for k in ("x",): d[k] = (d[k].astype(np.float32) * (1 / 1048576.0)).astype(d[k].dtype)
    return d
def setup_inputs_apart(rng):
    d = setup_inputs(rng)
    f = (10.0 ** rng.permutation(np.linspace(-1.5, 1.5, N))).astype(np.float32).reshape(N, 1, 1)
    for k in ("x",): d[k] = (d[k].astype(np.float32) * f).astype(d[k].dtype)
    return d
def reference(x, wv, wh):
    X, WV, WH = x.astype(np.float64), wv.astype(np.float64), wh.astype(np.float64)
    h = np.zeros((N, NB, 128, B))
    for r in range(N):
        for c in range(NB):
            a = X[r][:, B * c:B * c + B].copy()
            if r: a += WV[r].T @ h[r - 1][c]
            if c: a += WH[r].T @ h[r][c - 1]
            h[r][c] = np.maximum(a, 0.0)
    return {"y": np.concatenate([h[:, c] for c in range(NB)], axis=2).astype(ml_dtypes.bfloat16)}

@@ -1,0 +1,227 @@
+from concourse.mybir import AluOpType
+
+N, NB, B = 8, 6, 64
+WORLD = 512
+HW = NB * B
+WV0, WH0, X0, W = 0, 128, 256, 256 + HW
+
+GROUPS = [[0, 1, 2, 3], [4, 5, 6, 7]]
+ANCHOR = [0, 6]
+G = 2
+YSPLIT = {4: [(0, 2), (2, 6)], 6: [(0, 2), (2, 6)]}
+NE_IN1 = 8
+NE_IN2 = 8
+NE_H = 8
+NE_Y = 8
+K = max(len(q) for q in GROUPS)
+BANKS = 2 if 2 * K <= 8 else 1
+
+SCRATCH = {
+    "inp": ("sbuf", [128, K * W], "bfloat16"),
+    "hbuf": ("sbuf", [128, K * HW], "bfloat16"),
+    "up": ("sbuf", [128, HW], "bfloat16"),
+    "zero": ("sbuf", [128, B], "float32"),
+    "idz": ("sbuf", [128, 129], "bfloat16"),
+    "idd": ("dram", [129, 128], "bfloat16"),
+    "ident": ("sbuf", [128, 128], "bfloat16"),
+}
+for _i in range(K * BANKS):
+    SCRATCH["ps%d" % _i] = ("psum", [128, 512], "float32")
+
+SEMAPHORES = (["loaded", "rin", "sent", "stored", "fill", "ids1", "ids2"]
+              + ["in%d" % j for j in range(K)] + ["vd%d" % j for j in range(K)] + ["td%d" % j for j in range(K)]
+              + ["up%d" % m for m in range(NB // G)]
+              + ["y%d" % m for m in range(max([1] + [len(q) for q in YSPLIT.values()]))])
+
+PLAN = {}
+
+
+def ysplit(r):
+    return YSPLIT.get(r, [(0, NB)])
+
+
+def popcount(m):
+    return bin(m).count("1")
+
+
+def pick(m, n):
+    b = [i for i in range(m.bit_length()) if (m >> i) & 1][:n]
+    return sum(1 << i for i in b)
+
+
+def make_plan(T, topo):
+    if "p" in PLAN:
+        return PLAN["p"]
+    R = list(T.cores)
+
+    def near(a):
+        return [c for c in range(WORLD) if topo.host(c) == topo.host(a) and topo.chip(c) == topo.chip(a)
+                and topo.die(c) == topo.die(a)]
+
+    taken = set(R)
+    sites = [None] * len(GROUPS)
+    for s in reversed(range(len(GROUPS))):
+        need = [R[r] for r in GROUPS[s]] + ([sites[s + 1]] if s + 1 < len(GROUPS) else [])
+        sites[s] = [c for c in near(R[ANCHOR[s]]) if c not in taken and all(topo.may_write(c, d) for d in need)][0]
+        taken.add(sites[s])
+    relay, m_first, m_last, m_y, m_h = {}, {}, {}, {}, {}
+    for s, grp in enumerate(GROUPS):
+        dests = [R[r] for r in grp] + ([sites[s + 1]] if s + 1 < len(GROUPS) else [])
+        narrow = topo.mask(sites[s], dests[0])
+        for d in dests:
+            narrow &= topo.mask(sites[s], d)
+        for r in grp:
+            if topo.may_write(R[r], sites[s]):
+                m_last[r] = pick(topo.mask(R[r], sites[s]), NE_IN1)
+            else:
+                relay[r] = [c for c in near(R[r]) if c not in taken and topo.may_write(R[r], c)
+                            and topo.may_write(c, sites[s])][0]
+                taken.add(relay[r])
+                m_first[r] = pick(topo.mask(R[r], relay[r]), NE_IN1)
+                m_last[r] = pick(topo.mask(relay[r], sites[s]), NE_IN2)
+            wide = topo.mask(sites[s], R[r]) & ~narrow
+            own = s + 1 == len(GROUPS) and popcount(wide) >= NE_Y
+            m_y[r] = pick(wide if own else topo.mask(sites[s], R[r]), NE_Y)
+        if s + 1 < len(GROUPS):
+            m_h[s] = pick(topo.mask(sites[s], sites[s + 1]), NE_H)
+    PLAN["p"] = dict(R=R, sites=sites, relay=relay, m_first=m_first, m_last=m_last, m_y=m_y, m_h=m_h)
+    return PLAN["p"]
+
+
+def waiter(q, T):
+    seen = {}
+
+    def w(name, val):
+        if seen.get(name, 0) < val:
+            q.wait_ge(T.sem[name], val)
+            seen[name] = val
+    return w
+
+
+def send(g, T, topo, src, dst, out_ap, in_ap, sem, mask):
+    rid, pid = topo.addr(dst, src)
+    g.remote_dma(out_ap=out_ap, in_ap=in_ap, remote_sem=T.sem[sem], local_sem=T.sem.sent, pid=pid, routing_id=rid,
+                 dma_engine_mask=mask)
+    return popcount(mask)
+
+
+def rank_core(g, core, T, topo, P, r):
+    s = [i for i, q in enumerate(GROUPS) if r in q][0]
+    j = GROUPS[s].index(r)
+    lo = WV0 if r else WH0
+    n = 0
+    if r:
+        g.scalar.dma_start(T.inp[:, WV0:WV0 + 128], T.wv[:, :]).then_inc(T.sem.loaded, 16)
+        n += 16
+    g.sync.dma_start(T.inp[:, X0:W], T.x[:, :]).then_inc(T.sem.loaded, 16)
+    g.scalar.dma_start(T.inp[:, WH0:WH0 + 128], T.wh[:, :]).then_inc(T.sem.loaded, 16)
+    n += 32
+    g.wait_ge(T.sem.loaded, n)
+    if r in P["relay"]:
+        k = send(g, T, topo, core, P["relay"][r], T.inp[:, lo:W], T.inp[:, lo:W], "rin", P["m_first"][r])
+    else:
+        k = send(g, T, topo, core, P["sites"][s], T.inp[:, j * W + lo:j * W + W], T.inp[:, lo:W], "in%d" % j,
+                 P["m_last"][r])
+    g.wait_ge(T.sem.sent, k)
+    for m, (a, b) in enumerate(ysplit(r)):
+        g.sync.wait_ge(T.sem["y%d" % m], popcount(P["m_y"][r]))
+        g.sync.dma_start(T.y[:, B * a:B * b], T.hbuf[:, B * a:B * b]).then_inc(T.sem.stored, 16)
+    g.sync.wait_ge(T.sem.stored, 16 * len(ysplit(r)))
+
+
+def relay_core(g, core, T, topo, P, r):
+    s = [i for i, q in enumerate(GROUPS) if r in q][0]
+    j = GROUPS[s].index(r)
+    lo = WV0 if r else WH0
+    g.wait_ge(T.sem.rin, popcount(P["m_first"][r]))
+    k = send(g, T, topo, core, P["sites"][s], T.inp[:, j * W + lo:j * W + W], T.inp[:, lo:W], "in%d" % j,
+             P["m_last"][r])
+    g.wait_ge(T.sem.sent, k)
+
+
+def site_core(g, core, T, topo, P, s):
+    grp = GROUPS[s]
+    k = len(grp)
+    last = s + 1 == len(GROUPS)
+    g.vector.memset(T.idz[:, :], 0.0).then_inc(T.sem.fill, 1)
+    g.vector.memset(T.zero[:, :], 0.0).then_inc(T.sem.fill, 1)
+    g.vector.wait_ge(T.sem.fill, 2)
+    g.vector.memset(T.idz[:, 0:1], 1.0).then_inc(T.sem.fill, 1)
+    g.sync.wait_ge(T.sem.fill, 3)
+    g.sync.dma_start(T.idd[:, :], T.idz[:, :]).then_inc(T.sem.ids1, 16)
+    g.sync.wait_ge(T.sem.ids1, 16)
+    g.sync.dma_start(T.ident[:, :], T.idd[0:128, :]).then_inc(T.sem.ids2, 16)
+
+    early = 1 if (s == 0 and grp[0] not in P["relay"]) else 0
+    order = [(0, c) for c in range(NB)] if early else []
+    for d in range(k - early + NB - 1):
+        for j in reversed(range(early, k)):
+            c = d - (j - early)
+            if 0 <= c < NB:
+                order.append((j, c))
+    pos = dict((jc, i) for i, jc in enumerate(order))
+
+    def h(j, a, b):
+        return T.hbuf[:, j * HW + B * a:j * HW + B * b]
+
+    def bank(j, c):
+        return T["ps%d" % (j * BANKS + c % BANKS)][:, 0:B]
+
+    tw = waiter(g.tensor, T)
+    tw("ids2", 16)
+    for (j, c) in order:
+        r, base = grp[j], j * W
+        tw("in%d" % j, popcount(P["m_last"][r]))
+        if BANKS == 1 and c:
+            tw("vd%d" % j, c)
+        ops = [(T.ident[:, :], T.inp[:, base + X0 + B * c:base + X0 + B * c + B], None)]
+        if c:
+            ops.append((T.inp[:, base + WH0:base + WH0 + 128], h(j, c - 1, c), ("vd%d" % j, c)))
+        if r:
+            wv = T.inp[:, base + WV0:base + WV0 + 128]
+            if j:
+                ops.append((wv, h(j - 1, c, c + 1), ("vd%d" % (j - 1), c + 1)))
+            else:
+                ops.append((wv, T.up[:, B * c:B * c + B], ("up%d" % (c // G), popcount(P["m_h"][s - 1]))))
+        for i, (lhsT, rhs, wt) in enumerate(ops):
+            if wt:
+                tw(*wt)
+            ins = g.tensor.matmul(bank(j, c), lhsT, rhs, i == 0, i == len(ops) - 1)
+            if i == len(ops) - 1:
+                ins.then_inc(T.sem["td%d" % j], 1)
+
+    vw = waiter(g.vector, T)
+    for (j, c) in order:
+        vw("td%d" % j, c + 1)
+        g.vector.tensor_tensor(h(j, c, c + 1), bank(j, c), T.zero[:, :], AluOpType.max).then_inc(T.sem["vd%d" % j], 1)
+
+    msgs = []
+    if not last:
+        for m in range(NB // G):
+            msgs.append((pos[(k - 1, G * m + G - 1)], 0, k - 1, G * m, G * m + G, P["sites"][s + 1],
+                         T.up[:, B * G * m:B * G * (m + 1)], "up%d" % m, P["m_h"][s]))
+    first_h = min([q[0] for q in msgs]) if msgs else len(order)
+    for j, r in enumerate(grp):
+        for m, (a, b) in enumerate(ysplit(r)):
+            p = pos[(j, b - 1)]
+            msgs.append((p if (last or p < first_h) else len(order) + p, 1, j, a, b, P["R"][r],
+                         T.hbuf[:, B * a:B * b], "y%d" % m, P["m_y"][r]))
+    gw = waiter(g, T)
+    total = 0
+    for (_p, _q, j, a, b, dst, out_ap, sem, mask) in sorted(msgs, key=lambda q: (q[0], q[1], q[2])):
+        gw("vd%d" % j, b)
+        total += send(g, T, topo, core, dst, out_ap, h(j, a, b), sem, mask)
+    g.wait_ge(T.sem.sent, total)
+
+
+def rank_program(g, core, T, topo):
+    P = make_plan(T, topo)
+    r = T.rank_of(core)
+    if r is not None:
+        rank_core(g, core, T, topo, P, r)
+    elif core in P["sites"]:
+        site_core(g, core, T, topo, P, P["sites"].index(core))
+    else:
+        for q, c in P["relay"].items():
+            if c == core:
+                relay_core(g, core, T, topo, P, q)

@@ -1,20 +1,24 @@
+from concourse.bass import DstId, RemoteDMATransfer
 from concourse.mybir import AluOpType
 
 N, NB, B = 8, 6, 64
 WORLD = 512
 HW = NB * B
 WV0, WH0, X0, W = 0, 128, 256, 256 + HW
+REGIONS = [("wv", WV0, WH0), ("x", X0, W), ("wh", WH0, X0)]
 
 GROUPS = [[0, 1, 2, 3], [4, 5, 6, 7]]
 ANCHOR = [0, 6]
+CUTS = [W // 2, W]
 G = 2
-YSPLIT = {4: [(0, 2), (2, 6)], 6: [(0, 2), (2, 6)]}
+YSPLIT = {4: [(0, 2), (2, 6)], 6: [(0, 2), (2, 6)], 7: [(0, 2), (2, 6)]}
+RIDE = {6: 7}
 NE_IN1 = 8
 NE_IN2 = 8
 NE_H = 8
 NE_Y = 8
 K = max(len(q) for q in GROUPS)
-BANKS = 2 if 2 * K <= 8 else 1
+BANKS = 2
 
 SCRATCH = {
     "inp": ("sbuf", [128, K * W], "bfloat16"),
@@ -29,7 +33,8 @@ for _i in range(K * BANKS):
     SCRATCH["ps%d" % _i] = ("psum", [128, 512], "float32")
 
 SEMAPHORES = (["loaded", "rin", "sent", "stored", "fill", "ids1", "ids2"]
-              + ["in%d" % j for j in range(K)] + ["vd%d" % j for j in range(K)] + ["td%d" % j for j in range(K)]
+              + ["in%d_%d" % (j, i) for j in range(K) for i in range(len(CUTS))]
+              + ["td%d" % j for j in range(K)] + ["vd%d" % j for j in range(K)]
               + ["up%d" % m for m in range(NB // G)]
               + ["y%d" % m for m in range(max([1] + [len(q) for q in YSPLIT.values()]))])
 
@@ -44,8 +49,8 @@ def popcount(m):
     return bin(m).count("1")
 
 
-def pick(m, n):
-    b = [i for i in range(m.bit_length()) if (m >> i) & 1][:n]
+def pick(m, n, skip=0):
+    b = [i for i in range(m.bit_length()) if (m >> i) & 1][skip:skip + n]
     return sum(1 << i for i in b)
 
 
@@ -54,9 +59,14 @@ def make_plan(T, topo):
         return PLAN["p"]
     R = list(T.cores)
 
+    def on_chip(a):
+        return [c for c in range(WORLD) if topo.host(c) == topo.host(a) and topo.chip(c) == topo.chip(a)]
+
     def near(a):
-        return [c for c in range(WORLD) if topo.host(c) == topo.host(a) and topo.chip(c) == topo.chip(a)
-                and topo.die(c) == topo.die(a)]
+        return [c for c in on_chip(a) if topo.die(c) == topo.die(a)]
+
+    def far(a):
+        return [c for c in on_chip(a) if topo.die(c) != topo.die(a)]
 
     taken = set(R)
     sites = [None] * len(GROUPS)
@@ -74,11 +84,14 @@ def make_plan(T, topo):
             if topo.may_write(R[r], sites[s]):
                 m_last[r] = pick(topo.mask(R[r], sites[s]), NE_IN1)
             else:
-                relay[r] = [c for c in near(R[r]) if c not in taken and topo.may_write(R[r], c)
-                            and topo.may_write(c, sites[s])][0]
-                taken.add(relay[r])
-                m_first[r] = pick(topo.mask(R[r], relay[r]), NE_IN1)
-                m_last[r] = pick(topo.mask(relay[r], sites[s]), NE_IN2)
+                relay[r], m_first[r] = [], []
+                for i, spots in enumerate([near(R[r]), far(R[r])]):
+                    q = [c for c in spots if c not in taken and topo.may_write(R[r], c)
+                         and topo.may_write(c, sites[s])][0]
+                    taken.add(q)
+                    relay[r].append(q)
+                    m_first[r].append(pick(topo.mask(R[r], q), NE_IN1, i * NE_IN1))
+                    m_last[r] = pick(topo.mask(q, sites[s]), NE_IN2)
             wide = topo.mask(sites[s], R[r]) & ~narrow
             own = s + 1 == len(GROUPS) and popcount(wide) >= NE_Y
             m_y[r] = pick(wide if own else topo.mask(sites[s], R[r]), NE_Y)
@@ -86,6 +99,14 @@ def make_plan(T, topo):
             m_h[s] = pick(topo.mask(sites[s], sites[s + 1]), NE_H)
     PLAN["p"] = dict(R=R, sites=sites, relay=relay, m_first=m_first, m_last=m_last, m_y=m_y, m_h=m_h)
     return PLAN["p"]
+
+
+def pieces(P, r):
+    a, out = (WV0 if r else WH0), []
+    for b in (CUTS if r in P["relay"] else [W]):
+        out.append((a, b))
+        a = b
+    return out
 
 
 def waiter(q, T):
@@ -98,45 +119,54 @@ def waiter(q, T):
     return w
 
 
-def send(g, T, topo, src, dst, out_ap, in_ap, sem, mask):
-    rid, pid = topo.addr(dst, src)
-    g.remote_dma(out_ap=out_ap, in_ap=in_ap, remote_sem=T.sem[sem], local_sem=T.sem.sent, pid=pid, routing_id=rid,
-                 dma_engine_mask=mask)
-    return popcount(mask)
+def send(g, T, topo, src, items):
+    if len(items) == 1:
+        dst, out_ap, in_ap, sem, mask = items[0]
+        rid, pid = topo.addr(dst, src)
+        g.remote_dma(out_ap=out_ap, in_ap=in_ap, remote_sem=T.sem[sem], local_sem=T.sem.sent, pid=pid, routing_id=rid,
+                     dma_engine_mask=mask)
+    else:
+        trs = []
+        for (dst, out_ap, in_ap, sem, mask) in items:
+            rid, pid = topo.addr(dst, src)
+            trs.append(RemoteDMATransfer(dst_ids=[DstId(rid=rid, pnc=pid)], dma_engine_mask=mask,
+                                         remote_sem=T.sem[sem], src=in_ap, dst=out_ap))
+        g.remote_dma_fused(trs, local_sem=T.sem.sent)
+    return sum(popcount(q[4]) for q in items)
+
+
+def place(r):
+    s = [i for i, q in enumerate(GROUPS) if r in q][0]
+    return s, GROUPS[s].index(r)
 
 
 def rank_core(g, core, T, topo, P, r):
-    s = [i for i, q in enumerate(GROUPS) if r in q][0]
-    j = GROUPS[s].index(r)
-    lo = WV0 if r else WH0
-    n = 0
-    if r:
-        g.scalar.dma_start(T.inp[:, WV0:WV0 + 128], T.wv[:, :]).then_inc(T.sem.loaded, 16)
-        n += 16
-    g.sync.dma_start(T.inp[:, X0:W], T.x[:, :]).then_inc(T.sem.loaded, 16)
-    g.scalar.dma_start(T.inp[:, WH0:WH0 + 128], T.wh[:, :]).then_inc(T.sem.loaded, 16)
-    n += 32
-    g.wait_ge(T.sem.loaded, n)
+    s, j = place(r)
+    queues, n = [g.scalar, g.sync], 0
+    for (name, ra, rb) in REGIONS:
+        if r or name != "wv":
+            queues[n % 2 if r else (n + 1) % 2].dma_start(T.inp[:, ra:rb], T[name][:, :]).then_inc(T.sem.loaded, 16)
+            n += 1
+    g.wait_ge(T.sem.loaded, 16 * n)
     if r in P["relay"]:
-        k = send(g, T, topo, core, P["relay"][r], T.inp[:, lo:W], T.inp[:, lo:W], "rin", P["m_first"][r])
+        items = [(P["relay"][r][i], T.inp[:, a:b], T.inp[:, a:b], "rin", P["m_first"][r][i])
+                 for i, (a, b) in enumerate(pieces(P, r))]
     else:
-        k = send(g, T, topo, core, P["sites"][s], T.inp[:, j * W + lo:j * W + W], T.inp[:, lo:W], "in%d" % j,
-                 P["m_last"][r])
-    g.wait_ge(T.sem.sent, k)
+        items = [(P["sites"][s], T.inp[:, j * W + a:j * W + b], T.inp[:, a:b], "in%d_%d" % (j, i), P["m_last"][r])
+                 for i, (a, b) in enumerate(pieces(P, r))]
+    g.wait_ge(T.sem.sent, send(g, T, topo, core, items))
     for m, (a, b) in enumerate(ysplit(r)):
         g.sync.wait_ge(T.sem["y%d" % m], popcount(P["m_y"][r]))
         g.sync.dma_start(T.y[:, B * a:B * b], T.hbuf[:, B * a:B * b]).then_inc(T.sem.stored, 16)
     g.sync.wait_ge(T.sem.stored, 16 * len(ysplit(r)))
 
 
-def relay_core(g, core, T, topo, P, r):
-    s = [i for i, q in enumerate(GROUPS) if r in q][0]
-    j = GROUPS[s].index(r)
-    lo = WV0 if r else WH0
-    g.wait_ge(T.sem.rin, popcount(P["m_first"][r]))
-    k = send(g, T, topo, core, P["sites"][s], T.inp[:, j * W + lo:j * W + W], T.inp[:, lo:W], "in%d" % j,
-             P["m_last"][r])
-    g.wait_ge(T.sem.sent, k)
+def relay_core(g, core, T, topo, P, r, i):
+    s, j = place(r)
+    a, b = pieces(P, r)[i]
+    g.wait_ge(T.sem.rin, popcount(P["m_first"][r][i]))
+    g.wait_ge(T.sem.sent, send(g, T, topo, core, [(P["sites"][s], T.inp[:, j * W + a:j * W + b], T.inp[:, a:b],
+                                                   "in%d_%d" % (j, i), P["m_last"][r])]))
 
 
 def site_core(g, core, T, topo, P, s):
@@ -167,24 +197,27 @@ def site_core(g, core, T, topo, P, s):
     def bank(j, c):
         return T["ps%d" % (j * BANKS + c % BANKS)][:, 0:B]
 
+    def arrived(j, col):
+        r = grp[j]
+        i = [q for q, (a, b) in enumerate(pieces(P, r)) if a <= col < b][0]
+        return "in%d_%d" % (j, i), popcount(P["m_last"][r])
+
     tw = waiter(g.tensor, T)
     tw("ids2", 16)
     for (j, c) in order:
         r, base = grp[j], j * W
-        tw("in%d" % j, popcount(P["m_last"][r]))
-        if BANKS == 1 and c:
-            tw("vd%d" % j, c)
-        ops = [(T.ident[:, :], T.inp[:, base + X0 + B * c:base + X0 + B * c + B], None)]
+        ops = [(T.ident[:, :], T.inp[:, base + X0 + B * c:base + X0 + B * c + B], [arrived(j, X0 + B * c)])]
         if c:
-            ops.append((T.inp[:, base + WH0:base + WH0 + 128], h(j, c - 1, c), ("vd%d" % j, c)))
+            ops.append((T.inp[:, base + WH0:base + WH0 + 128], h(j, c - 1, c), [arrived(j, WH0), ("vd%d" % j, c)]))
         if r:
             wv = T.inp[:, base + WV0:base + WV0 + 128]
             if j:
-                ops.append((wv, h(j - 1, c, c + 1), ("vd%d" % (j - 1), c + 1)))
+                ops.append((wv, h(j - 1, c, c + 1), [arrived(j, WV0), ("vd%d" % (j - 1), c + 1)]))
             else:
-                ops.append((wv, T.up[:, B * c:B * c + B], ("up%d" % (c // G), popcount(P["m_h"][s - 1]))))
-        for i, (lhsT, rhs, wt) in enumerate(ops):
-            if wt:
+                ops.append((wv, T.up[:, B * c:B * c + B],
+                            [arrived(j, WV0), ("up%d" % (c // G), popcount(P["m_h"][s - 1]))]))
+        for i, (lhsT, rhs, wts) in enumerate(ops):
+            for wt in wts:
                 tw(*wt)
             ins = g.tensor.matmul(bank(j, c), lhsT, rhs, i == 0, i == len(ops) - 1)
             if i == len(ops) - 1:
@@ -195,22 +228,31 @@ def site_core(g, core, T, topo, P, s):
         vw("td%d" % j, c + 1)
         g.vector.tensor_tensor(h(j, c, c + 1), bank(j, c), T.zero[:, :], AluOpType.max).then_inc(T.sem["vd%d" % j], 1)
 
-    msgs = []
+    calls = {}
     if not last:
         for m in range(NB // G):
-            msgs.append((pos[(k - 1, G * m + G - 1)], 0, k - 1, G * m, G * m + G, P["sites"][s + 1],
-                         T.up[:, B * G * m:B * G * (m + 1)], "up%d" % m, P["m_h"][s]))
-    first_h = min([q[0] for q in msgs]) if msgs else len(order)
-    for j, r in enumerate(grp):
+            calls[("h", m)] = [pos[(k - 1, G * m + G - 1)], 0, [(k - 1, G * m + G)],
+                               [(P["sites"][s + 1], T.up[:, B * G * m:B * G * (m + 1)], h(k - 1, G * m, G * m + G),
+                                 "up%d" % m, P["m_h"][s])]]
+    first_h = min([q[0] for q in calls.values()]) if calls else len(order)
+    for j, r in sorted(enumerate(grp), key=lambda q: q[1] in RIDE):
         for m, (a, b) in enumerate(ysplit(r)):
             p = pos[(j, b - 1)]
-            msgs.append((p if (last or p < first_h) else len(order) + p, 1, j, a, b, P["R"][r],
-                         T.hbuf[:, B * a:B * b], "y%d" % m, P["m_y"][r]))
+            p = p if (last or p < first_h) else len(order) + p
+            item = (P["R"][r], T.hbuf[:, B * a:B * b], h(j, a, b), "y%d" % m, P["m_y"][r])
+            if r in RIDE:
+                q = calls[(RIDE[r], m)]
+                q[0] = max(q[0], p)
+                q[2].append((j, b))
+                q[3].append(item)
+            else:
+                calls[(r, m)] = [p, 1, [(j, b)], [item]]
     gw = waiter(g, T)
     total = 0
-    for (_p, _q, j, a, b, dst, out_ap, sem, mask) in sorted(msgs, key=lambda q: (q[0], q[1], q[2])):
-        gw("vd%d" % j, b)
-        total += send(g, T, topo, core, dst, out_ap, h(j, a, b), sem, mask)
+    for (_p, _q, waits, items) in sorted(calls.values(), key=lambda q: (q[0], q[1], q[2])):
+        for (j, b) in waits:
+            gw("vd%d" % j, b)
+        total += send(g, T, topo, core, items)
     g.wait_ge(T.sem.sent, total)
 
 
@@ -222,6 +264,7 @@ def rank_program(g, core, T, topo):
     elif core in P["sites"]:
         site_core(g, core, T, topo, P, P["sites"].index(core))
     else:
-        for q, c in P["relay"].items():
-            if c == core:
-                relay_core(g, core, T, topo, P, q)
+        for q, cs in P["relay"].items():
+            for i, c in enumerate(cs):
+                if c == core:
+                    relay_core(g, core, T, topo, P, q, i)

@@ -8,14 +8,13 @@ WV0, WH0, X0, W = 0, 128, 256, 256 + HW
 REGIONS = [("wv", WV0, WH0), ("x", X0, W), ("wh", WH0, X0)]
 
 GROUPS = [[0, 1, 2, 3], [4, 5, 6, 7]]
-ANCHOR = [0, 6]
-CUTS = [W // 2, W]
+ANCHOR = [0, 1, 2, 3]
 G = 2
-YSPLIT = {4: [(0, 2), (2, 6)], 6: [(0, 2), (2, 6)], 7: [(0, 2), (2, 6)]}
-RIDE = {6: 7}
-NE_IN1 = 8
-NE_IN2 = 8
-NE_H = 8
+RET = {0: [(0, 0, 3, 0)],
+       1: [(1, 0, 1, 0), (1, 1, 6, 1)],
+       2: [(0, 3, 6, 1), (2, 0, 6, 0)],
+       3: [(3, 0, 6, 0)]}
+STORE = [(0, 4), (4, 6)]
 NE_Y = 8
 K = max(len(q) for q in GROUPS)
 BANKS = 2
@@ -25,24 +24,19 @@ SCRATCH = {
     "hbuf": ("sbuf", [128, K * HW], "bfloat16"),
     "up": ("sbuf", [128, HW], "bfloat16"),
     "zero": ("sbuf", [128, B], "float32"),
-    "idz": ("sbuf", [128, 129], "bfloat16"),
-    "idd": ("dram", [129, 128], "bfloat16"),
+    "ones": ("sbuf", [128, 128], "bfloat16"),
     "ident": ("sbuf", [128, 128], "bfloat16"),
 }
 for _i in range(K * BANKS):
     SCRATCH["ps%d" % _i] = ("psum", [128, 512], "float32")
 
-SEMAPHORES = (["loaded", "rin", "sent", "stored", "fill", "ids1", "ids2"]
-              + ["in%d_%d" % (j, i) for j in range(K) for i in range(len(CUTS))]
+SEMAPHORES = (["loaded", "rin", "sent", "stored", "fill", "idn"]
+              + ["in%d_%d" % (j, i) for j in range(K) for i in range(2)]
               + ["td%d" % j for j in range(K)] + ["vd%d" % j for j in range(K)]
               + ["up%d" % m for m in range(NB // G)]
-              + ["y%d" % m for m in range(max([1] + [len(q) for q in YSPLIT.values()]))])
+              + ["y%d" % m for m in range(2)])
 
 PLAN = {}
-
-
-def ysplit(r):
-    return YSPLIT.get(r, [(0, NB)])
 
 
 def popcount(m):
@@ -54,59 +48,109 @@ def pick(m, n, skip=0):
     return sum(1 << i for i in b)
 
 
+def place(r):
+    s = [i for i, q in enumerate(GROUPS) if r in q][0]
+    return s, GROUPS[s].index(r)
+
+
 def make_plan(T, topo):
     if "p" in PLAN:
         return PLAN["p"]
     R = list(T.cores)
 
+    def same_chip(a, b):
+        return topo.host(a) == topo.host(b) and topo.chip(a) == topo.chip(b)
+
     def on_chip(a):
-        return [c for c in range(WORLD) if topo.host(c) == topo.host(a) and topo.chip(c) == topo.chip(a)]
-
-    def near(a):
-        return [c for c in on_chip(a) if topo.die(c) == topo.die(a)]
-
-    def far(a):
-        return [c for c in on_chip(a) if topo.die(c) != topo.die(a)]
+        return [c for c in range(WORLD) if same_chip(a, c)]
 
     taken = set(R)
-    sites = [None] * len(GROUPS)
-    for s in reversed(range(len(GROUPS))):
-        need = [R[r] for r in GROUPS[s]] + ([sites[s + 1]] if s + 1 < len(GROUPS) else [])
-        sites[s] = [c for c in near(R[ANCHOR[s]]) if c not in taken and all(topo.may_write(c, d) for d in need)][0]
-        taken.add(sites[s])
-    relay, m_first, m_last, m_y, m_h = {}, {}, {}, {}, {}
-    for s, grp in enumerate(GROUPS):
-        dests = [R[r] for r in grp] + ([sites[s + 1]] if s + 1 < len(GROUPS) else [])
-        narrow = topo.mask(sites[s], dests[0])
-        for d in dests:
-            narrow &= topo.mask(sites[s], d)
-        for r in grp:
-            if topo.may_write(R[r], sites[s]):
-                m_last[r] = pick(topo.mask(R[r], sites[s]), NE_IN1)
-            else:
-                relay[r], m_first[r] = [], []
-                for i, spots in enumerate([near(R[r]), far(R[r])]):
-                    q = [c for c in spots if c not in taken and topo.may_write(R[r], c)
-                         and topo.may_write(c, sites[s])][0]
-                    taken.add(q)
-                    relay[r].append(q)
-                    m_first[r].append(pick(topo.mask(R[r], q), NE_IN1, i * NE_IN1))
-                    m_last[r] = pick(topo.mask(q, sites[s]), NE_IN2)
-            wide = topo.mask(sites[s], R[r]) & ~narrow
-            own = s + 1 == len(GROUPS) and popcount(wide) >= NE_Y
-            m_y[r] = pick(wide if own else topo.mask(sites[s], R[r]), NE_Y)
-        if s + 1 < len(GROUPS):
-            m_h[s] = pick(topo.mask(sites[s], sites[s + 1]), NE_H)
-    PLAN["p"] = dict(R=R, sites=sites, relay=relay, m_first=m_first, m_last=m_last, m_y=m_y, m_h=m_h)
+    sites = []
+    for a in ANCHOR:
+        cand = [c for c in on_chip(R[a]) if topo.die(c) == topo.die(R[a]) and c not in taken]
+        best = max(cand, key=lambda c: (sum(1 for d in R if topo.may_write(c, d)), -c))
+        sites.append(best)
+        taken.add(best)
+    feeds = dict((s, []) for s in range(len(sites)))
+    ahead = [topo.may_write(R[0], c) for c in sites]
+    for r in reversed(GROUPS[1]):
+        s = [q for q in sorted(range(len(sites)), key=lambda q: (not ahead[q], q))
+             if not feeds[q] and topo.may_write(sites[q], R[r])][0]
+        feeds[s].append(R[r])
+    urgent = dict((sites[s], feeds[s][0] in [R[q] for q in GROUPS[1][len(GROUPS[1]) // 2:]]) for s in feeds)
+    m_h = {}
+    for s, ds in feeds.items():
+        for n, d in enumerate(ds):
+            m = topo.mask(sites[s], d)
+            m_h[d] = pick(m, popcount(m) // len(ds), n * (popcount(m) // len(ds)))
+
+    dests = {}
+    for r in range(N):
+        gi, j = place(r)
+        dests[r] = list(sites) if gi == 0 else [R[q] for q in GROUPS[1] if q > r]
+
+    sends, relays, arrive, pcs = {}, {}, {}, {}
+    for r in range(N):
+        src = R[r]
+        gi, j = place(r)
+        direct = [d for d in dests[r] if topo.may_write(src, d)]
+        rest = [d for d in dests[r] if not topo.may_write(src, d)]
+        a = WV0 if r else WH0
+        pcs[r] = [(a, (a + W) // 2), ((a + W) // 2, W)] if rest else [(a, W)]
+        if gi == 0:
+            pcs[r].append((a, W))
+            parts = [len(pcs[r]) - 1]
+            rest = sorted(rest, key=lambda d: not urgent[d])
+        else:
+            parts = list(range(len(pcs[r])))
+        straight = [(d, i, j * W, "in%d_%d" % (j, n)) for d in direct for n, i in enumerate(parts)]
+        passed, hops = [], []
+        for i in range(2 if rest else 0):
+            q = [c for c in on_chip(src) if c not in taken and (topo.die(c) == topo.die(src)) == (i == 0)
+                 and topo.may_write(src, c) and all(topo.may_write(c, d) for d in rest)][0]
+            taken.add(q)
+            passed.append((q, i, 0, "rin"))
+            hops.append((q, i, rest))
+        lots = [passed, straight] if gi == 0 else [straight + passed]
+        sends[r], got = [], {}
+        for targets in lots:
+            off = [t for t in targets if not same_chip(src, t[0])]
+            on = [t for t in targets if same_chip(src, t[0])]
+            narrow = 0
+            if off:
+                narrow = topo.mask(src, off[0][0])
+                for t in off:
+                    narrow &= topo.mask(src, t[0])
+            call = []
+            for lot, pool in ((off, narrow), (on, (topo.mask(src, on[0][0]) & ~narrow) if on else 0)):
+                for n, t in enumerate(lot):
+                    ne = popcount(pool) // len(lot)
+                    call.append(t + (pick(pool, ne, n * ne),))
+                    got[(t[0], t[1])] = ne
+            if call:
+                sends[r].append(call)
+        for d in direct:
+            arrive[(d, r)] = [(pcs[r][i][0], pcs[r][i][1], "in%d_%d" % (j, n), got[(d, i)])
+                              for n, i in enumerate(parts)]
+        for (q, i, ds) in hops:
+            outs = []
+            for n, d in enumerate(ds):
+                m = topo.mask(q, d)
+                ne = popcount(m) // (1 if gi == 0 else len(ds))
+                outs.append((d, j * W, "in%d_%d" % (j, i), pick(m, ne, 0 if gi == 0 else n * ne)))
+                arrive.setdefault((d, r), []).append((pcs[r][i][0], pcs[r][i][1], "in%d_%d" % (j, i), ne))
+            relays[q] = (r, i, got[(q, i)], outs, gi == 0)
+
+    m_y = {}
+    for s, lst in RET.items():
+        narrow = topo.mask(sites[s], feeds[s][0])
+        for (r, a, b, m) in lst:
+            full = topo.mask(sites[s], R[r])
+            wide = full & ~narrow
+            m_y[(r, m)] = pick(wide if (r and b == NB and popcount(wide) >= NE_Y) else full, NE_Y)
+    PLAN["p"] = dict(R=R, sites=sites, feeds=feeds, ahead=ahead, m_h=m_h, sends=sends, relays=relays, arrive=arrive,
+                     pcs=pcs, m_y=m_y)
     return PLAN["p"]
-
-
-def pieces(P, r):
-    a, out = (WV0 if r else WH0), []
-    for b in (CUTS if r in P["relay"] else [W]):
-        out.append((a, b))
-        a = b
-    return out
 
 
 def waiter(q, T):
@@ -135,54 +179,19 @@ def send(g, T, topo, src, items):
     return sum(popcount(q[4]) for q in items)
 
 
-def place(r):
-    s = [i for i, q in enumerate(GROUPS) if r in q][0]
-    return s, GROUPS[s].index(r)
+def h_ap(T, j, a, b):
+    return T.hbuf[:, j * HW + B * a:j * HW + B * b]
 
 
-def rank_core(g, core, T, topo, P, r):
-    s, j = place(r)
-    queues, n = [g.scalar, g.sync], 0
-    for (name, ra, rb) in REGIONS:
-        if r or name != "wv":
-            queues[n % 2 if r else (n + 1) % 2].dma_start(T.inp[:, ra:rb], T[name][:, :]).then_inc(T.sem.loaded, 16)
-            n += 1
-    g.wait_ge(T.sem.loaded, 16 * n)
-    if r in P["relay"]:
-        items = [(P["relay"][r][i], T.inp[:, a:b], T.inp[:, a:b], "rin", P["m_first"][r][i])
-                 for i, (a, b) in enumerate(pieces(P, r))]
-    else:
-        items = [(P["sites"][s], T.inp[:, j * W + a:j * W + b], T.inp[:, a:b], "in%d_%d" % (j, i), P["m_last"][r])
-                 for i, (a, b) in enumerate(pieces(P, r))]
-    g.wait_ge(T.sem.sent, send(g, T, topo, core, items))
-    for m, (a, b) in enumerate(ysplit(r)):
-        g.sync.wait_ge(T.sem["y%d" % m], popcount(P["m_y"][r]))
-        g.sync.dma_start(T.y[:, B * a:B * b], T.hbuf[:, B * a:B * b]).then_inc(T.sem.stored, 16)
-    g.sync.wait_ge(T.sem.stored, 16 * len(ysplit(r)))
-
-
-def relay_core(g, core, T, topo, P, r, i):
-    s, j = place(r)
-    a, b = pieces(P, r)[i]
-    g.wait_ge(T.sem.rin, popcount(P["m_first"][r][i]))
-    g.wait_ge(T.sem.sent, send(g, T, topo, core, [(P["sites"][s], T.inp[:, j * W + a:j * W + b], T.inp[:, a:b],
-                                                   "in%d_%d" % (j, i), P["m_last"][r])]))
-
-
-def site_core(g, core, T, topo, P, s):
-    grp = GROUPS[s]
-    k = len(grp)
-    last = s + 1 == len(GROUPS)
-    g.vector.memset(T.idz[:, :], 0.0).then_inc(T.sem.fill, 1)
+def constants(g, T):
+    g.vector.memset(T.ones[:, :], 1.0).then_inc(T.sem.fill, 1)
     g.vector.memset(T.zero[:, :], 0.0).then_inc(T.sem.fill, 1)
-    g.vector.wait_ge(T.sem.fill, 2)
-    g.vector.memset(T.idz[:, 0:1], 1.0).then_inc(T.sem.fill, 1)
-    g.sync.wait_ge(T.sem.fill, 3)
-    g.sync.dma_start(T.idd[:, :], T.idz[:, :]).then_inc(T.sem.ids1, 16)
-    g.sync.wait_ge(T.sem.ids1, 16)
-    g.sync.dma_start(T.ident[:, :], T.idd[0:128, :]).then_inc(T.sem.ids2, 16)
+    g.wait_ge(T.sem.fill, 2)
+    g.affine_select(T.ident[:, :], T.ones[:, :], [[-1, 128]], AluOpType.is_equal, 0.0, 0, 1).then_inc(T.sem.idn, 1)
 
-    early = 1 if (s == 0 and grp[0] not in P["relay"]) else 0
+
+def wave(g, core, T, P, grp, early, own):
+    k = len(grp)
     order = [(0, c) for c in range(NB)] if early else []
     for d in range(k - early + NB - 1):
         for j in reversed(range(early, k)):
@@ -191,31 +200,31 @@ def site_core(g, core, T, topo, P, s):
                 order.append((j, c))
     pos = dict((jc, i) for i, jc in enumerate(order))
 
-    def h(j, a, b):
-        return T.hbuf[:, j * HW + B * a:j * HW + B * b]
-
     def bank(j, c):
         return T["ps%d" % (j * BANKS + c % BANKS)][:, 0:B]
 
     def arrived(j, col):
         r = grp[j]
-        i = [q for q, (a, b) in enumerate(pieces(P, r)) if a <= col < b][0]
-        return "in%d_%d" % (j, i), popcount(P["m_last"][r])
+        if own and own[0] == r:
+            return own[1], own[2]
+        q = [t for t in P["arrive"][(core, r)] if t[0] <= col < t[1]][0]
+        return q[2], q[3]
 
     tw = waiter(g.tensor, T)
-    tw("ids2", 16)
+    tw("idn", 1)
     for (j, c) in order:
         r, base = grp[j], j * W
         ops = [(T.ident[:, :], T.inp[:, base + X0 + B * c:base + X0 + B * c + B], [arrived(j, X0 + B * c)])]
         if c:
-            ops.append((T.inp[:, base + WH0:base + WH0 + 128], h(j, c - 1, c), [arrived(j, WH0), ("vd%d" % j, c)]))
+            ops.append((T.inp[:, base + WH0:base + WH0 + 128], h_ap(T, j, c - 1, c),
+                        [arrived(j, WH0), ("vd%d" % j, c)]))
         if r:
             wv = T.inp[:, base + WV0:base + WV0 + 128]
             if j:
-                ops.append((wv, h(j - 1, c, c + 1), [arrived(j, WV0), ("vd%d" % (j - 1), c + 1)]))
+                ops.append((wv, h_ap(T, j - 1, c, c + 1), [arrived(j, WV0), ("vd%d" % (j - 1), c + 1)]))
             else:
                 ops.append((wv, T.up[:, B * c:B * c + B],
-                            [arrived(j, WV0), ("up%d" % (c // G), popcount(P["m_h"][s - 1]))]))
+                            [arrived(j, WV0), ("up%d" % (c // G), popcount(P["m_h"][core]))]))
         for i, (lhsT, rhs, wts) in enumerate(ops):
             for wt in wts:
                 tw(*wt)
@@ -224,32 +233,85 @@ def site_core(g, core, T, topo, P, s):
                 ins.then_inc(T.sem["td%d" % j], 1)
 
     vw = waiter(g.vector, T)
+    vw("fill", 2)
     for (j, c) in order:
         vw("td%d" % j, c + 1)
-        g.vector.tensor_tensor(h(j, c, c + 1), bank(j, c), T.zero[:, :], AluOpType.max).then_inc(T.sem["vd%d" % j], 1)
+        g.vector.tensor_tensor(h_ap(T, j, c, c + 1), bank(j, c), T.zero[:, :],
+                               AluOpType.max).then_inc(T.sem["vd%d" % j], 1)
+    return pos
 
-    calls = {}
-    if not last:
-        for m in range(NB // G):
-            calls[("h", m)] = [pos[(k - 1, G * m + G - 1)], 0, [(k - 1, G * m + G)],
-                               [(P["sites"][s + 1], T.up[:, B * G * m:B * G * (m + 1)], h(k - 1, G * m, G * m + G),
-                                 "up%d" % m, P["m_h"][s])]]
-    first_h = min([q[0] for q in calls.values()]) if calls else len(order)
-    for j, r in sorted(enumerate(grp), key=lambda q: q[1] in RIDE):
-        for m, (a, b) in enumerate(ysplit(r)):
-            p = pos[(j, b - 1)]
-            p = p if (last or p < first_h) else len(order) + p
-            item = (P["R"][r], T.hbuf[:, B * a:B * b], h(j, a, b), "y%d" % m, P["m_y"][r])
-            if r in RIDE:
-                q = calls[(RIDE[r], m)]
-                q[0] = max(q[0], p)
-                q[2].append((j, b))
-                q[3].append(item)
-            else:
-                calls[(r, m)] = [p, 1, [(j, b)], [item]]
+
+def rank_core(g, core, T, topo, P, r):
+    gi, j = place(r)
+    base = j * W if gi else 0
+    queues, n = [g.scalar, g.sync], 0
+    for (name, ra, rb) in REGIONS:
+        if r or name != "wv":
+            queues[n % 2 if r else (n + 1) % 2].dma_start(T.inp[:, base + ra:base + rb],
+                                                          T[name][:, :]).then_inc(T.sem.loaded, 16)
+            n += 1
+    if gi:
+        constants(g, T)
+    g.wait_ge(T.sem.loaded, 16 * n)
+    total = 0
+    for call in P["sends"][r]:
+        items = []
+        for (dst, i, col, sem, mask) in call:
+            a, b = P["pcs"][r][i]
+            items.append((dst, T.inp[:, col + a:col + b], T.inp[:, base + a:base + b], sem, mask))
+        total += send(g, T, topo, core, items)
+    if total:
+        g.wait_ge(T.sem.sent, total)
+    if gi:
+        wave(g, core, T, P, GROUPS[gi][:j + 1], 0, (r, "loaded", 16 * n))
+        for (a, b) in STORE:
+            g.sync.wait_ge(T.sem["vd%d" % j], b)
+            g.sync.dma_start(T.y[:, B * a:B * b], h_ap(T, j, a, b)).then_inc(T.sem.stored, 16)
+        g.sync.wait_ge(T.sem.stored, 16 * len(STORE))
+    else:
+        back = sorted((m, a, b) for lst in RET.values() for (q, a, b, m) in lst if q == r)
+        for (m, a, b) in back:
+            g.sync.wait_ge(T.sem["y%d" % m], popcount(P["m_y"][(r, m)]))
+            g.sync.dma_start(T.y[:, B * a:B * b], T.hbuf[:, B * a:B * b]).then_inc(T.sem.stored, 16)
+        g.sync.wait_ge(T.sem.stored, 16 * len(back))
+
+
+def relay_core(g, core, T, topo, P):
+    r, i, count, outs, apart = P["relays"][core]
+    a, b = P["pcs"][r][i]
+    items = [(d, T.inp[:, col + a:col + b], T.inp[:, a:b], sem, mask) for (d, col, sem, mask) in outs]
+    g.wait_ge(T.sem.rin, count)
+    total = 0
+    for call in ([[q] for q in items] if apart else [items]):
+        total += send(g, T, topo, core, call)
+    g.wait_ge(T.sem.sent, total)
+
+
+def site_core(g, core, T, topo, P, s):
+    grp = GROUPS[0]
+    k = len(grp)
+    constants(g, T)
+    pos = wave(g, core, T, P, grp, 1 if P["ahead"][s] else 0, None)
+    calls = []
+    for m in range(NB // G):
+        calls.append([pos[(k - 1, G * m + G - 1)], [(k - 1, G * m + G)],
+                      [(d, T.up[:, B * G * m:B * G * (m + 1)], h_ap(T, k - 1, G * m, G * m + G), "up%d" % m,
+                        P["m_h"][d]) for d in P["feeds"][s]]])
+    first_h = min(q[0] for q in calls)
+    late = [len(pos), [], []]
+    for (r, a, b, m) in RET[s]:
+        j = grp.index(r)
+        item = (P["R"][r], T.hbuf[:, B * a:B * b], h_ap(T, j, a, b), "y%d" % m, P["m_y"][(r, m)])
+        if pos[(j, b - 1)] < first_h:
+            calls.append([pos[(j, b - 1)], [(j, b)], [item]])
+        else:
+            late[1].append((j, b))
+            late[2].append(item)
+    if late[2]:
+        calls.append(late)
     gw = waiter(g, T)
     total = 0
-    for (_p, _q, waits, items) in sorted(calls.values(), key=lambda q: (q[0], q[1], q[2])):
+    for (_p, waits, items) in sorted(calls, key=lambda q: q[0]):
         for (j, b) in waits:
             gw("vd%d" % j, b)
         total += send(g, T, topo, core, items)
@@ -263,8 +325,5 @@ def rank_program(g, core, T, topo):
         rank_core(g, core, T, topo, P, r)
     elif core in P["sites"]:
         site_core(g, core, T, topo, P, P["sites"].index(core))
-    else:
-        for q, cs in P["relay"].items():
-            for i, c in enumerate(cs):
-                if c == core:
-                    relay_core(g, core, T, topo, P, q, i)
+    elif core in P["relays"]:
+        relay_core(g, core, T, topo, P)

from concourse.bass import DstId, RemoteDMATransfer
from concourse.mybir import AluOpType

N, NB, B = 8, 6, 64
WORLD = 512
HW = NB * B
WV0, WH0, X0, W = 0, 128, 256, 256 + HW
REGIONS = [("wv", WV0, WH0), ("x", X0, W), ("wh", WH0, X0)]

GROUPS = [[0, 1, 2, 3], [4, 5, 6, 7]]
ANCHOR = [0, 1, 2, 3]
G = 2
RET = {0: [(0, 0, 3, 0)],
       1: [(1, 0, 1, 0), (1, 1, 6, 1)],
       2: [(0, 3, 6, 1), (2, 0, 6, 0)],
       3: [(3, 0, 6, 0)]}
STORE = [(0, 4), (4, 6)]
NE_Y = 8
K = max(len(q) for q in GROUPS)
BANKS = 2

SCRATCH = {
    "inp": ("sbuf", [128, K * W], "bfloat16"),
    "hbuf": ("sbuf", [128, K * HW], "bfloat16"),
    "up": ("sbuf", [128, HW], "bfloat16"),
    "zero": ("sbuf", [128, B], "float32"),
    "ones": ("sbuf", [128, 128], "bfloat16"),
    "ident": ("sbuf", [128, 128], "bfloat16"),
}
for _i in range(K * BANKS):
    SCRATCH["ps%d" % _i] = ("psum", [128, 512], "float32")

SEMAPHORES = (["loaded", "rin", "sent", "stored", "fill", "idn"]
              + ["in%d_%d" % (j, i) for j in range(K) for i in range(2)]
              + ["td%d" % j for j in range(K)] + ["vd%d" % j for j in range(K)]
              + ["up%d" % m for m in range(NB // G)]
              + ["y%d" % m for m in range(2)])

PLAN = {}


def popcount(m):
    return bin(m).count("1")


def pick(m, n, skip=0):
    b = [i for i in range(m.bit_length()) if (m >> i) & 1][skip:skip + n]
    return sum(1 << i for i in b)


def place(r):
    s = [i for i, q in enumerate(GROUPS) if r in q][0]
    return s, GROUPS[s].index(r)


def make_plan(T, topo):
    if "p" in PLAN:
        return PLAN["p"]
    R = list(T.cores)

    def same_chip(a, b):
        return topo.host(a) == topo.host(b) and topo.chip(a) == topo.chip(b)

    def on_chip(a):
        return [c for c in range(WORLD) if same_chip(a, c)]

    taken = set(R)
    sites = []
    for a in ANCHOR:
        cand = [c for c in on_chip(R[a]) if topo.die(c) == topo.die(R[a]) and c not in taken]
        best = max(cand, key=lambda c: (sum(1 for d in R if topo.may_write(c, d)), -c))
        sites.append(best)
        taken.add(best)
    feeds = dict((s, []) for s in range(len(sites)))
    ahead = [topo.may_write(R[0], c) for c in sites]
    for r in reversed(GROUPS[1]):
        s = [q for q in sorted(range(len(sites)), key=lambda q: (not ahead[q], q))
             if not feeds[q] and topo.may_write(sites[q], R[r])][0]
        feeds[s].append(R[r])
    urgent = dict((sites[s], feeds[s][0] in [R[q] for q in GROUPS[1][len(GROUPS[1]) // 2:]]) for s in feeds)
    m_h = {}
    for s, ds in feeds.items():
        for n, d in enumerate(ds):
            m = topo.mask(sites[s], d)
            m_h[d] = pick(m, popcount(m) // len(ds), n * (popcount(m) // len(ds)))

    dests = {}
    for r in range(N):
        gi, j = place(r)
        dests[r] = list(sites) if gi == 0 else [R[q] for q in GROUPS[1] if q > r]

    sends, relays, arrive, pcs = {}, {}, {}, {}
    for r in range(N):
        src = R[r]
        gi, j = place(r)
        direct = [d for d in dests[r] if topo.may_write(src, d)]
        rest = [d for d in dests[r] if not topo.may_write(src, d)]
        a = WV0 if r else WH0
        pcs[r] = [(a, (a + W) // 2), ((a + W) // 2, W)] if rest else [(a, W)]
        if gi == 0:
            pcs[r].append((a, W))
            parts = [len(pcs[r]) - 1]
            rest = sorted(rest, key=lambda d: not urgent[d])
        else:
            parts = list(range(len(pcs[r])))
        straight = [(d, i, j * W, "in%d_%d" % (j, n)) for d in direct for n, i in enumerate(parts)]
        passed, hops = [], []
        for i in range(2 if rest else 0):
            q = [c for c in on_chip(src) if c not in taken and (topo.die(c) == topo.die(src)) == (i == 0)
                 and topo.may_write(src, c) and all(topo.may_write(c, d) for d in rest)][0]
            taken.add(q)
            passed.append((q, i, 0, "rin"))
            hops.append((q, i, rest))
        lots = [passed, straight] if gi == 0 else [straight + passed]
        sends[r], got = [], {}
        for targets in lots:
            off = [t for t in targets if not same_chip(src, t[0])]
            on = [t for t in targets if same_chip(src, t[0])]
            narrow = 0
            if off:
                narrow = topo.mask(src, off[0][0])
                for t in off:
                    narrow &= topo.mask(src, t[0])
            call = []
            for lot, pool in ((off, narrow), (on, (topo.mask(src, on[0][0]) & ~narrow) if on else 0)):
                for n, t in enumerate(lot):
                    ne = popcount(pool) // len(lot)
                    call.append(t + (pick(pool, ne, n * ne),))
                    got[(t[0], t[1])] = ne
            if call:
                sends[r].append(call)
        for d in direct:
            arrive[(d, r)] = [(pcs[r][i][0], pcs[r][i][1], "in%d_%d" % (j, n), got[(d, i)])
                              for n, i in enumerate(parts)]
        for (q, i, ds) in hops:
            outs = []
            for n, d in enumerate(ds):
                m = topo.mask(q, d)
                ne = popcount(m) // (1 if gi == 0 else len(ds))
                outs.append((d, j * W, "in%d_%d" % (j, i), pick(m, ne, 0 if gi == 0 else n * ne)))
                arrive.setdefault((d, r), []).append((pcs[r][i][0], pcs[r][i][1], "in%d_%d" % (j, i), ne))
            relays[q] = (r, i, got[(q, i)], outs, gi == 0)

    m_y = {}
    for s, lst in RET.items():
        narrow = topo.mask(sites[s], feeds[s][0])
        for (r, a, b, m) in lst:
            full = topo.mask(sites[s], R[r])
            wide = full & ~narrow
            m_y[(r, m)] = pick(wide if (r and b == NB and popcount(wide) >= NE_Y) else full, NE_Y)
    PLAN["p"] = dict(R=R, sites=sites, feeds=feeds, ahead=ahead, m_h=m_h, sends=sends, relays=relays, arrive=arrive,
                     pcs=pcs, m_y=m_y)
    return PLAN["p"]


def waiter(q, T):
    seen = {}

    def w(name, val):
        if seen.get(name, 0) < val:
            q.wait_ge(T.sem[name], val)
            seen[name] = val
    return w


def send(g, T, topo, src, items):
    if len(items) == 1:
        dst, out_ap, in_ap, sem, mask = items[0]
        rid, pid = topo.addr(dst, src)
        g.remote_dma(out_ap=out_ap, in_ap=in_ap, remote_sem=T.sem[sem], local_sem=T.sem.sent, pid=pid, routing_id=rid,
                     dma_engine_mask=mask)
    else:
        trs = []
        for (dst, out_ap, in_ap, sem, mask) in items:
            rid, pid = topo.addr(dst, src)
            trs.append(RemoteDMATransfer(dst_ids=[DstId(rid=rid, pnc=pid)], dma_engine_mask=mask,
                                         remote_sem=T.sem[sem], src=in_ap, dst=out_ap))
        g.remote_dma_fused(trs, local_sem=T.sem.sent)
    return sum(popcount(q[4]) for q in items)


def h_ap(T, j, a, b):
    return T.hbuf[:, j * HW + B * a:j * HW + B * b]


def constants(g, T):
    g.vector.memset(T.ones[:, :], 1.0).then_inc(T.sem.fill, 1)
    g.vector.memset(T.zero[:, :], 0.0).then_inc(T.sem.fill, 1)
    g.wait_ge(T.sem.fill, 2)
    g.affine_select(T.ident[:, :], T.ones[:, :], [[-1, 128]], AluOpType.is_equal, 0.0, 0, 1).then_inc(T.sem.idn, 1)


def wave(g, core, T, P, grp, early, own):
    k = len(grp)
    order = [(0, c) for c in range(NB)] if early else []
    for d in range(k - early + NB - 1):
        for j in reversed(range(early, k)):
            c = d - (j - early)
            if 0 <= c < NB:
                order.append((j, c))
    pos = dict((jc, i) for i, jc in enumerate(order))

    def bank(j, c):
        return T["ps%d" % (j * BANKS + c % BANKS)][:, 0:B]

    def arrived(j, col):
        r = grp[j]
        if own and own[0] == r:
            return own[1], own[2]
        q = [t for t in P["arrive"][(core, r)] if t[0] <= col < t[1]][0]
        return q[2], q[3]

    tw = waiter(g.tensor, T)
    tw("idn", 1)
    for (j, c) in order:
        r, base = grp[j], j * W
        ops = [(T.ident[:, :], T.inp[:, base + X0 + B * c:base + X0 + B * c + B], [arrived(j, X0 + B * c)])]
        if c:
            ops.append((T.inp[:, base + WH0:base + WH0 + 128], h_ap(T, j, c - 1, c),
                        [arrived(j, WH0), ("vd%d" % j, c)]))
        if r:
            wv = T.inp[:, base + WV0:base + WV0 + 128]
            if j:
                ops.append((wv, h_ap(T, j - 1, c, c + 1), [arrived(j, WV0), ("vd%d" % (j - 1), c + 1)]))
            else:
                ops.append((wv, T.up[:, B * c:B * c + B],
                            [arrived(j, WV0), ("up%d" % (c // G), popcount(P["m_h"][core]))]))
        for i, (lhsT, rhs, wts) in enumerate(ops):
            for wt in wts:
                tw(*wt)
            ins = g.tensor.matmul(bank(j, c), lhsT, rhs, i == 0, i == len(ops) - 1)
            if i == len(ops) - 1:
                ins.then_inc(T.sem["td%d" % j], 1)

    vw = waiter(g.vector, T)
    vw("fill", 2)
    for (j, c) in order:
        vw("td%d" % j, c + 1)
        g.vector.tensor_tensor(h_ap(T, j, c, c + 1), bank(j, c), T.zero[:, :],
                               AluOpType.max).then_inc(T.sem["vd%d" % j], 1)
    return pos


def rank_core(g, core, T, topo, P, r):
    gi, j = place(r)
    base = j * W if gi else 0
    queues, n = [g.scalar, g.sync], 0
    for (name, ra, rb) in REGIONS:
        if r or name != "wv":
            queues[n % 2 if r else (n + 1) % 2].dma_start(T.inp[:, base + ra:base + rb],
                                                          T[name][:, :]).then_inc(T.sem.loaded, 16)
            n += 1
    if gi:
        constants(g, T)
    g.wait_ge(T.sem.loaded, 16 * n)
    total = 0
    for call in P["sends"][r]:
        items = []
        for (dst, i, col, sem, mask) in call:
            a, b = P["pcs"][r][i]
            items.append((dst, T.inp[:, col + a:col + b], T.inp[:, base + a:base + b], sem, mask))
        total += send(g, T, topo, core, items)
    if total:
        g.wait_ge(T.sem.sent, total)
    if gi:
        wave(g, core, T, P, GROUPS[gi][:j + 1], 0, (r, "loaded", 16 * n))
        for (a, b) in STORE:
            g.sync.wait_ge(T.sem["vd%d" % j], b)
            g.sync.dma_start(T.y[:, B * a:B * b], h_ap(T, j, a, b)).then_inc(T.sem.stored, 16)
        g.sync.wait_ge(T.sem.stored, 16 * len(STORE))
    else:
        back = sorted((m, a, b) for lst in RET.values() for (q, a, b, m) in lst if q == r)
        for (m, a, b) in back:
            g.sync.wait_ge(T.sem["y%d" % m], popcount(P["m_y"][(r, m)]))
            g.sync.dma_start(T.y[:, B * a:B * b], T.hbuf[:, B * a:B * b]).then_inc(T.sem.stored, 16)
        g.sync.wait_ge(T.sem.stored, 16 * len(back))


def relay_core(g, core, T, topo, P):
    r, i, count, outs, apart = P["relays"][core]
    a, b = P["pcs"][r][i]
    items = [(d, T.inp[:, col + a:col + b], T.inp[:, a:b], sem, mask) for (d, col, sem, mask) in outs]
    g.wait_ge(T.sem.rin, count)
    total = 0
    for call in ([[q] for q in items] if apart else [items]):
        total += send(g, T, topo, core, call)
    g.wait_ge(T.sem.sent, total)


def site_core(g, core, T, topo, P, s):
    grp = GROUPS[0]
    k = len(grp)
    constants(g, T)
    pos = wave(g, core, T, P, grp, 1 if P["ahead"][s] else 0, None)
    calls = []
    for m in range(NB // G):
        calls.append([pos[(k - 1, G * m + G - 1)], [(k - 1, G * m + G)],
                      [(d, T.up[:, B * G * m:B * G * (m + 1)], h_ap(T, k - 1, G * m, G * m + G), "up%d" % m,
                        P["m_h"][d]) for d in P["feeds"][s]]])
    first_h = min(q[0] for q in calls)
    late = [len(pos), [], []]
    for (r, a, b, m) in RET[s]:
        j = grp.index(r)
        item = (P["R"][r], T.hbuf[:, B * a:B * b], h_ap(T, j, a, b), "y%d" % m, P["m_y"][(r, m)])
        if pos[(j, b - 1)] < first_h:
            calls.append([pos[(j, b - 1)], [(j, b)], [item]])
        else:
            late[1].append((j, b))
            late[2].append(item)
    if late[2]:
        calls.append(late)
    gw = waiter(g, T)
    total = 0
    for (_p, waits, items) in sorted(calls, key=lambda q: q[0]):
        for (j, b) in waits:
            gw("vd%d" % j, b)
        total += send(g, T, topo, core, items)
    g.wait_ge(T.sem.sent, total)


def rank_program(g, core, T, topo):
    P = make_plan(T, topo)
    r = T.rank_of(core)
    if r is not None:
        rank_core(g, core, T, topo, P, r)
    elif core in P["sites"]:
        site_core(g, core, T, topo, P, P["sites"].index(core))
    elif core in P["relays"]:
        relay_core(g, core, T, topo, P)
